import numpy as np
import ml_dtypes


def mxq(x, axis, fmt="e4m3"):
    dtype, down = {"e4m3": (ml_dtypes.float8_e4m3fn, 7), "e5m2": (ml_dtypes.float8_e5m2, 14)}[fmt]
    v = np.moveaxis(np.asarray(x, np.float32).astype(ml_dtypes.bfloat16).astype(np.float64), axis, -1)
    blocks = v.reshape(v.shape[:-1] + (-1, 32))
    amax = np.abs(blocks).max(-1, keepdims=True)
    byte = np.maximum(np.where(amax > 0, np.frexp(amax)[1] - 1 + 127, 0) - down, 1)
    scale = np.exp2(byte - 127.0)
    codes = (blocks / scale).astype(np.float32).astype(dtype).astype(np.float64)
    return np.moveaxis((codes * scale).reshape(v.shape), -1, axis)


WIDE = False


def mx_kscale(k, group=512):
    if not WIDE:
        return np.ones(k)
    levels = np.array([18, -18])
    if group != 512:
        return np.exp2(np.random.permutation(np.resize(levels, k // group))).repeat(group)
    if k % 512:
        return np.exp2(np.random.permutation(np.resize(levels, k // 32))).repeat(32)
    a = np.empty((k // 512, 16))
    for p in range(k // 512):
        a[p, :8] = np.random.permutation(np.resize(levels, 8))
        for g in range(8):
            far = levels[np.abs(levels - a[p, g]) >= 10]
            a[p, g + 8] = far[np.random.randint(len(far))]
    return np.exp2(a.ravel()).repeat(32)


def f64(x):
    return np.asarray(x).astype(np.float64)


G, D, M, N = 4, 128, 256, 512


def setup_inputs():
    n = np.random.standard_normal
    s = mx_kscale(D, 0)[:, None]
    return {
        "x": (n((G, D, N)) * s).astype(np.float32),
        "w": (n((G, D, M)) / np.sqrt(D) / s).astype(np.float32),
        "u": (n((G, D, M)) / np.sqrt(D) / s).astype(np.float32),
    }


def reference(x, w, u):
    xq = mxq(f64(x), 1, "e4m3")
    h = mxq(f64(w), 1, "e4m3").transpose(0, 2, 1) @ xq
    g = mxq(f64(u), 1, "e4m3").transpose(0, 2, 1) @ xq
    y = np.maximum(h, 0.0) * g
    return y

@@ -1,0 +1,118 @@
+from contextlib import ExitStack
+
+import concourse.mybir as mybir
+
+G, D, M, N = 4, 128, 256, 512
+FLOPS = 2 * 2 * G * D * M * N
+
+F32 = mybir.dt.float32
+BF16 = mybir.dt.bfloat16
+U32 = mybir.dt.uint32
+U8 = mybir.dt.uint8
+FP8X4 = mybir.dt.float8_e4m3fn_x4
+ALU = mybir.AluOpType
+
+P = 128
+PACK = 4
+ROWS = D // PACK
+M_TILE = 128
+RUN = 4
+X_SPLIT = 352
+
+
+def interleave_views(grouped, raw, c0, c1):
+    dst = grouped[:, PACK * c0 : PACK * c1].rearrange("p (c i t) -> p c t i", i=RUN, t=PACK)
+    src = raw[:, :, c0:c1].rearrange("p t (c i) -> p c t i", i=RUN)
+    return dst, src
+
+
+def tile_rows_gglu_relu_kernel(tc, x, w, u, out):
+    nc = tc.nc
+    halves = M // M_TILE
+
+    with ExitStack() as ctx:
+        keep = ctx.enter_context(tc.tile_pool(name="keep", bufs=1))
+        psum = ctx.enter_context(tc.psum_pool(name="psum", bufs=1))
+        ctx.enter_context(tc.manual_schedule())
+
+        def operand(name, width):
+            return {
+                "raw": keep.tile([P, PACK, width], F32, name=name + "_raw", align_bytes=64),
+                "grouped": keep.tile([P, PACK * width], BF16, name=name + "_grouped", align_bytes=64),
+                "codes": keep.tile([P, width], U32, name=name + "_codes", align_bytes=64),
+                "scales": keep.tile([P, width], U8, name=name + "_scales", align_bytes=64),
+            }
+
+        xo = operand("x", N)
+        uo = [operand("u%d" % h, M_TILE) for h in range(halves)]
+        wo = [operand("w%d" % h, M_TILE) for h in range(halves)]
+        gate_bank = [psum.tile([P, N], F32, name="gate_bank%d" % g) for g in range(G)]
+        relu_bank = [psum.tile([P, N], F32, name="relu_bank%d" % g) for g in range(G)]
+        gate = [[keep.tile([P, N], F32, name="gate%d_%d" % (h, g)) for g in range(G)] for h in range(halves)]
+        res = [[keep.tile([P, N], F32, name="res%d_%d" % (h, g)) for g in range(G)] for h in range(halves)]
+
+        def load(op, src, c0, c1):
+            nc.sync.dma_start(out=op["raw"][:], in_=src.rearrange("g (p j) c -> (g p) j c", j=PACK)[:, :, c0:c1])
+
+        def quantize(op):
+            nc.vector.quantize_mx(out=op["codes"][:].bitcast(FP8X4), scales=op["scales"][:], in_=op["grouped"][:])
+
+        def products(banks, op):
+            for g in range(G):
+                product(banks, op, g)
+
+        def product(banks, op, g):
+            rows = slice(ROWS * g, ROWS * (g + 1))
+            nc.tensor.matmul_mx(
+                out=banks[g][:],
+                lhsT=op["codes"][rows, :].bitcast(FP8X4),
+                lhsT_scale=op["scales"][rows, :],
+                rhs=xo["codes"][rows, :].bitcast(FP8X4),
+                rhs_scale=xo["scales"][rows, :],
+                start=True,
+                stop=True,
+            )
+
+        def finish(h, g):
+            nc.vector.scalar_tensor_tensor(
+                out=res[h][g][:], in0=relu_bank[g][:], scalar=0.0, in1=gate[h][g][:], op0=ALU.max, op1=ALU.mult
+            )
+            nc.sync.dma_start(out=out[g, M_TILE * h : M_TILE * (h + 1), :], in_=res[h][g][:])
+
+        load(xo, x, 0, N)
+        for h in range(halves):
+            load(uo[h], u, M_TILE * h, M_TILE * (h + 1))
+            load(wo[h], w, M_TILE * h, M_TILE * (h + 1))
+
+        dst, src = interleave_views(xo["grouped"], xo["raw"], 0, X_SPLIT)
+        nc.vector.tensor_copy(out=dst, in_=src)
+        dst, src = interleave_views(xo["grouped"], xo["raw"], X_SPLIT, N)
+        nc.scalar.copy(out=dst, in_=src)
+        dst, src = interleave_views(uo[0]["grouped"], uo[0]["raw"], 0, M_TILE)
+        nc.scalar.copy(out=dst, in_=src)
+        quantize(xo)
+        quantize(uo[0])
+        products(gate_bank, uo[0])
+        dst, src = interleave_views(wo[0]["grouped"], wo[0]["raw"], 0, M_TILE)
+        nc.vector.tensor_copy(out=dst, in_=src)
+        quantize(wo[0])
+        products(relu_bank, wo[0])
+        dst, src = interleave_views(uo[1]["grouped"], uo[1]["raw"], 0, M_TILE)
+        nc.vector.tensor_copy(out=dst, in_=src)
+        quantize(uo[1])
+
+        for g in range(G):
+            nc.scalar.copy(out=gate[0][g][:], in_=gate_bank[g][:])
+            if g == 1:
+                dst, src = interleave_views(wo[1]["grouped"], wo[1]["raw"], 0, M_TILE)
+                nc.scalar.copy(out=dst, in_=src)
+            finish(0, g)
+            if g == 1:
+                quantize(wo[1])
+            product(gate_bank, uo[1], g)
+            if g >= 1:
+                product(relu_bank, wo[1], g - 1)
+        product(relu_bank, wo[1], G - 1)
+        for g in range(G):
+            nc.scalar.copy(out=gate[1][g][:], in_=gate_bank[g][:])
+            finish(1, g)

@@ -17,7 +17,7 @@ PACK = 4
 ROWS = D // PACK
 M_TILE = 128
 RUN = 4
-X_SPLIT = 352
+X_SCALAR = 192
 
 
 def interleave_views(grouped, raw, c0, c1):
@@ -73,46 +73,79 @@ def tile_rows_gglu_relu_kernel(tc, x, w, u, out):
                 stop=True,
             )
 
-        def finish(h, g):
-            nc.vector.scalar_tensor_tensor(
-                out=res[h][g][:], in0=relu_bank[g][:], scalar=0.0, in1=gate[h][g][:], op0=ALU.max, op1=ALU.mult
+        def finish(h, g, pieces=1):
+            width = N // pieces
+            for c0 in range(0, N, width):
+                cols = slice(c0, c0 + width)
+                nc.vector.scalar_tensor_tensor(
+                    out=res[h][g][:, cols],
+                    in0=relu_bank[g][:, cols],
+                    scalar=0.0,
+                    in1=gate[h][g][:, cols],
+                    op0=ALU.max,
+                    op1=ALU.mult,
+                )
+                nc.sync.dma_start(out=out[g, M_TILE * h : M_TILE * (h + 1), cols], in_=res[h][g][:, cols])
+
+        def vector_interleave(op, c0, c1):
+            dst, src = interleave_views(op["grouped"], op["raw"], c0, c1)
+            nc.vector.tensor_copy(out=dst, in_=src)
+
+        def scalar_interleave(op, c0, c1):
+            dst, src = interleave_views(op["grouped"], op["raw"], c0, c1)
+            nc.scalar.copy(out=dst, in_=src)
+
+        def quantize_window(op, c0, c1):
+            nc.vector.quantize_mx(
+                out=op["codes"][:, c0:c1].bitcast(FP8X4),
+                scales=op["scales"][:, c0:c1],
+                in_=op["grouped"][:, PACK * c0 : PACK * c1],
             )
-            nc.sync.dma_start(out=out[g, M_TILE * h : M_TILE * (h + 1), :], in_=res[h][g][:])
+
+        def copy_gate(h, g):
+            nc.scalar.copy(out=gate[h][g][:], in_=gate_bank[g][:])
 
         load(xo, x, 0, N)
         for h in range(halves):
             load(uo[h], u, M_TILE * h, M_TILE * (h + 1))
             load(wo[h], w, M_TILE * h, M_TILE * (h + 1))
 
-        dst, src = interleave_views(xo["grouped"], xo["raw"], 0, X_SPLIT)
-        nc.vector.tensor_copy(out=dst, in_=src)
-        dst, src = interleave_views(xo["grouped"], xo["raw"], X_SPLIT, N)
-        nc.scalar.copy(out=dst, in_=src)
-        dst, src = interleave_views(uo[0]["grouped"], uo[0]["raw"], 0, M_TILE)
-        nc.scalar.copy(out=dst, in_=src)
-        quantize(xo)
+        mid = N // 2
+        half = M_TILE // 2
+        vector_interleave(xo, 0, mid)
+        scalar_interleave(xo, mid, mid + X_SCALAR)
+        vector_interleave(xo, mid + X_SCALAR, N)
+        scalar_interleave(uo[0], 0, M_TILE)
+        quantize_window(xo, 0, mid)
+        quantize_window(xo, mid, N)
         quantize(uo[0])
         products(gate_bank, uo[0])
-        dst, src = interleave_views(wo[0]["grouped"], wo[0]["raw"], 0, M_TILE)
-        nc.vector.tensor_copy(out=dst, in_=src)
+        vector_interleave(wo[0], 0, half)
+        scalar_interleave(wo[0], half, M_TILE)
         quantize(wo[0])
         products(relu_bank, wo[0])
-        dst, src = interleave_views(uo[1]["grouped"], uo[1]["raw"], 0, M_TILE)
-        nc.vector.tensor_copy(out=dst, in_=src)
-        quantize(uo[1])
+        vector_interleave(uo[1], 0, M_TILE)
 
+        copy_gate(0, 0)
+        finish(0, 0, 2)
+        quantize(uo[1])
+        copy_gate(0, 1)
+        product(gate_bank, uo[1], 0)
+        product(gate_bank, uo[1], 1)
+        vector_interleave(wo[1], 0, half)
+        scalar_interleave(wo[1], half, M_TILE)
+        finish(0, 1)
+        quantize(wo[1])
+        copy_gate(0, 2)
+        product(gate_bank, uo[1], 2)
+        product(relu_bank, wo[1], 0)
+        product(relu_bank, wo[1], 1)
+        finish(0, 2)
+        copy_gate(0, 3)
+        product(gate_bank, uo[1], 3)
+        product(relu_bank, wo[1], 2)
+        finish(0, 3)
+        product(relu_bank, wo[1], 3)
         for g in range(G):
-            nc.scalar.copy(out=gate[0][g][:], in_=gate_bank[g][:])
-            if g == 1:
-                dst, src = interleave_views(wo[1]["grouped"], wo[1]["raw"], 0, M_TILE)
-                nc.scalar.copy(out=dst, in_=src)
-            finish(0, g)
-            if g == 1:
-                quantize(wo[1])
-            product(gate_bank, uo[1], g)
-            if g >= 1:
-                product(relu_bank, wo[1], g - 1)
-        product(relu_bank, wo[1], G - 1)
-        for g in range(G):
-            nc.scalar.copy(out=gate[1][g][:], in_=gate_bank[g][:])
-            finish(1, g)
+            copy_gate(1, g)
+            finish(1, g, 2 if g == G - 1 else 1)

@@ -44,8 +44,8 @@ def tile_rows_gglu_relu_kernel(tc, x, w, u, out):
             }
 
         xo = operand("x", N)
-        uo = [operand("u%d" % h, M_TILE) for h in range(halves)]
-        wo = [operand("w%d" % h, M_TILE) for h in range(halves)]
+        uo = operand("u", M)
+        wo = operand("w", M)
         gate_bank = [psum.tile([P, N], F32, name="gate_bank%d" % g) for g in range(G)]
         relu_bank = [psum.tile([P, N], F32, name="relu_bank%d" % g) for g in range(G)]
         gate = [[keep.tile([P, N], F32, name="gate%d_%d" % (h, g)) for g in range(G)] for h in range(halves)]
@@ -54,19 +54,17 @@ def tile_rows_gglu_relu_kernel(tc, x, w, u, out):
         def load(op, src, c0, c1):
             nc.sync.dma_start(out=op["raw"][:], in_=src.rearrange("g (p j) c -> (g p) j c", j=PACK)[:, :, c0:c1])
 
-        def quantize(op):
-            nc.vector.quantize_mx(out=op["codes"][:].bitcast(FP8X4), scales=op["scales"][:], in_=op["grouped"][:])
-
-        def products(banks, op):
+        def products(banks, op, h):
             for g in range(G):
-                product(banks, op, g)
+                product(banks, op, h, g)
 
-        def product(banks, op, g):
+        def product(banks, op, h, g):
             rows = slice(ROWS * g, ROWS * (g + 1))
+            cols = slice(M_TILE * h, M_TILE * (h + 1))
             nc.tensor.matmul_mx(
                 out=banks[g][:],
-                lhsT=op["codes"][rows, :].bitcast(FP8X4),
-                lhsT_scale=op["scales"][rows, :],
+                lhsT=op["codes"][rows, cols].bitcast(FP8X4),
+                lhsT_scale=op["scales"][rows, cols],
                 rhs=xo["codes"][rows, :].bitcast(FP8X4),
                 rhs_scale=xo["scales"][rows, :],
                 start=True,
@@ -106,46 +104,34 @@ def tile_rows_gglu_relu_kernel(tc, x, w, u, out):
             nc.scalar.copy(out=gate[h][g][:], in_=gate_bank[g][:])
 
         load(xo, x, 0, N)
-        for h in range(halves):
-            load(uo[h], u, M_TILE * h, M_TILE * (h + 1))
-            load(wo[h], w, M_TILE * h, M_TILE * (h + 1))
+        load(uo, u, 0, M)
+        load(wo, w, 0, M)
 
         mid = N // 2
         half = M_TILE // 2
         vector_interleave(xo, 0, mid)
         scalar_interleave(xo, mid, mid + X_SCALAR)
         vector_interleave(xo, mid + X_SCALAR, N)
-        scalar_interleave(uo[0], 0, M_TILE)
         quantize_window(xo, 0, mid)
         quantize_window(xo, mid, N)
-        quantize(uo[0])
-        products(gate_bank, uo[0])
-        vector_interleave(wo[0], 0, half)
-        scalar_interleave(wo[0], half, M_TILE)
-        quantize(wo[0])
-        products(relu_bank, wo[0])
-        vector_interleave(uo[1], 0, M_TILE)
+        scalar_interleave(uo, 0, M_TILE)
+        vector_interleave(uo, M_TILE, M)
+        quantize_window(uo, 0, M_TILE)
+        products(gate_bank, uo, 0)
+        quantize_window(uo, M_TILE, M)
+        vector_interleave(wo, 0, half)
+        scalar_interleave(wo, half, M_TILE)
+        quantize_window(wo, 0, M_TILE)
+        products(relu_bank, wo, 0)
+        vector_interleave(wo, M_TILE, M)
 
-        copy_gate(0, 0)
-        finish(0, 0, 2)
-        quantize(uo[1])
-        copy_gate(0, 1)
-        product(gate_bank, uo[1], 0)
-        product(gate_bank, uo[1], 1)
-        vector_interleave(wo[1], 0, half)
-        scalar_interleave(wo[1], half, M_TILE)
-        finish(0, 1)
-        quantize(wo[1])
-        copy_gate(0, 2)
-        product(gate_bank, uo[1], 2)
-        product(relu_bank, wo[1], 0)
-        product(relu_bank, wo[1], 1)
-        finish(0, 2)
-        copy_gate(0, 3)
-        product(gate_bank, uo[1], 3)
-        product(relu_bank, wo[1], 2)
-        finish(0, 3)
-        product(relu_bank, wo[1], 3)
+        for g in range(G):
+            copy_gate(0, g)
+            product(gate_bank, uo, 1, g)
+            finish(0, g, 2 if g == 0 else 1)
+            if g == 0:
+                quantize_window(wo, M_TILE, M)
+            product(relu_bank, wo, 1, g)
         for g in range(G):
             copy_gate(1, g)
-            finish(1, g, 2 if g == G - 1 else 1)
+            finish(1, g)

from contextlib import ExitStack

import concourse.mybir as mybir

G, D, M, N = 4, 128, 256, 512
FLOPS = 2 * 2 * G * D * M * N

F32 = mybir.dt.float32
BF16 = mybir.dt.bfloat16
U32 = mybir.dt.uint32
U8 = mybir.dt.uint8
FP8X4 = mybir.dt.float8_e4m3fn_x4
ALU = mybir.AluOpType

P = 128
PACK = 4
ROWS = D // PACK
M_TILE = 128
RUN = 4
X_SCALAR = 192


def interleave_views(grouped, raw, c0, c1):
    dst = grouped[:, PACK * c0 : PACK * c1].rearrange("p (c i t) -> p c t i", i=RUN, t=PACK)
    src = raw[:, :, c0:c1].rearrange("p t (c i) -> p c t i", i=RUN)
    return dst, src


def tile_rows_gglu_relu_kernel(tc, x, w, u, out):
    nc = tc.nc
    halves = M // M_TILE

    with ExitStack() as ctx:
        keep = ctx.enter_context(tc.tile_pool(name="keep", bufs=1))
        psum = ctx.enter_context(tc.psum_pool(name="psum", bufs=1))
        ctx.enter_context(tc.manual_schedule())

        def operand(name, width):
            return {
                "raw": keep.tile([P, PACK, width], F32, name=name + "_raw", align_bytes=64),
                "grouped": keep.tile([P, PACK * width], BF16, name=name + "_grouped", align_bytes=64),
                "codes": keep.tile([P, width], U32, name=name + "_codes", align_bytes=64),
                "scales": keep.tile([P, width], U8, name=name + "_scales", align_bytes=64),
            }

        xo = operand("x", N)
        uo = operand("u", M)
        wo = operand("w", M)
        gate_bank = [psum.tile([P, N], F32, name="gate_bank%d" % g) for g in range(G)]
        relu_bank = [psum.tile([P, N], F32, name="relu_bank%d" % g) for g in range(G)]
        gate = [[keep.tile([P, N], F32, name="gate%d_%d" % (h, g)) for g in range(G)] for h in range(halves)]
        res = [[keep.tile([P, N], F32, name="res%d_%d" % (h, g)) for g in range(G)] for h in range(halves)]

        def load(op, src, c0, c1):
            nc.sync.dma_start(out=op["raw"][:], in_=src.rearrange("g (p j) c -> (g p) j c", j=PACK)[:, :, c0:c1])

        def products(banks, op, h):
            for g in range(G):
                product(banks, op, h, g)

        def product(banks, op, h, g):
            rows = slice(ROWS * g, ROWS * (g + 1))
            cols = slice(M_TILE * h, M_TILE * (h + 1))
            nc.tensor.matmul_mx(
                out=banks[g][:],
                lhsT=op["codes"][rows, cols].bitcast(FP8X4),
                lhsT_scale=op["scales"][rows, cols],
                rhs=xo["codes"][rows, :].bitcast(FP8X4),
                rhs_scale=xo["scales"][rows, :],
                start=True,
                stop=True,
            )

        def finish(h, g, pieces=1):
            width = N // pieces
            for c0 in range(0, N, width):
                cols = slice(c0, c0 + width)
                nc.vector.scalar_tensor_tensor(
                    out=res[h][g][:, cols],
                    in0=relu_bank[g][:, cols],
                    scalar=0.0,
                    in1=gate[h][g][:, cols],
                    op0=ALU.max,
                    op1=ALU.mult,
                )
                nc.sync.dma_start(out=out[g, M_TILE * h : M_TILE * (h + 1), cols], in_=res[h][g][:, cols])

        def vector_interleave(op, c0, c1):
            dst, src = interleave_views(op["grouped"], op["raw"], c0, c1)
            nc.vector.tensor_copy(out=dst, in_=src)

        def scalar_interleave(op, c0, c1):
            dst, src = interleave_views(op["grouped"], op["raw"], c0, c1)
            nc.scalar.copy(out=dst, in_=src)

        def quantize_window(op, c0, c1):
            nc.vector.quantize_mx(
                out=op["codes"][:, c0:c1].bitcast(FP8X4),
                scales=op["scales"][:, c0:c1],
                in_=op["grouped"][:, PACK * c0 : PACK * c1],
            )

        def copy_gate(h, g):
            nc.scalar.copy(out=gate[h][g][:], in_=gate_bank[g][:])

        load(xo, x, 0, N)
        load(uo, u, 0, M)
        load(wo, w, 0, M)

        mid = N // 2
        half = M_TILE // 2
        vector_interleave(xo, 0, mid)
        scalar_interleave(xo, mid, mid + X_SCALAR)
        vector_interleave(xo, mid + X_SCALAR, N)
        quantize_window(xo, 0, mid)
        quantize_window(xo, mid, N)
        scalar_interleave(uo, 0, M_TILE)
        vector_interleave(uo, M_TILE, M)
        quantize_window(uo, 0, M_TILE)
        products(gate_bank, uo, 0)
        quantize_window(uo, M_TILE, M)
        vector_interleave(wo, 0, half)
        scalar_interleave(wo, half, M_TILE)
        quantize_window(wo, 0, M_TILE)
        products(relu_bank, wo, 0)
        vector_interleave(wo, M_TILE, M)

        for g in range(G):
            copy_gate(0, g)
            product(gate_bank, uo, 1, g)
            finish(0, g, 2 if g == 0 else 1)
            if g == 0:
                quantize_window(wo, M_TILE, M)
            product(relu_bank, wo, 1, g)
        for g in range(G):
            copy_gate(1, g)
            finish(1, g)
